import numpy as np
import ml_dtypes


def mxq(x, axis, fmt="e4m3"):
    dtype, down = {"e4m3": (ml_dtypes.float8_e4m3fn, 7), "e5m2": (ml_dtypes.float8_e5m2, 14)}[fmt]
    v = np.moveaxis(np.asarray(x, np.float32).astype(ml_dtypes.bfloat16).astype(np.float64), axis, -1)
    blocks = v.reshape(v.shape[:-1] + (-1, 32))
    amax = np.abs(blocks).max(-1, keepdims=True)
    byte = np.maximum(np.where(amax > 0, np.frexp(amax)[1] - 1 + 127, 0) - down, 1)
    scale = np.exp2(byte - 127.0)
    codes = (blocks / scale).astype(np.float32).astype(dtype).astype(np.float64)
    return np.moveaxis((codes * scale).reshape(v.shape), -1, axis)


WIDE = False


def mx_kscale(k):
    if not WIDE:
        return np.ones(k)
    levels = np.array([10, -10, 5, -5, 0])
    if k % 512:
        return np.exp2(np.random.permutation(np.resize(levels, k // 32))).repeat(32)
    a = np.empty((k // 512, 16))
    for p in range(k // 512):
        a[p, :8] = np.random.permutation(np.resize(levels, 8))
        for g in range(8):
            far = levels[np.abs(levels - a[p, g]) >= 10]
            a[p, g + 8] = far[np.random.randint(len(far))]
    return np.exp2(a.ravel()).repeat(32)


def f64(x):
    return np.asarray(x).astype(np.float64)


def striped(idx):
    return np.tile(idx.reshape(-1, 16).T, (8, 1)).astype(np.uint16)


def unstriped(offs):
    return offs[:16].T.reshape(-1).astype(np.int64)


E2M1 = np.array([0.0, 0.5, 1.0, 1.5, 2.0, 3.0, 4.0, 6.0, -0.0, -0.5, -1.0, -1.5, -2.0, -3.0, -4.0, -6.0])


def pack_weight(w, fmt):
    k, n = w.shape
    w = f64(np.asarray(w, np.float32).astype(ml_dtypes.bfloat16)).reshape(k // 32, 32, n)
    amax = np.abs(w).max(1)
    if fmt == "e4m3":
        byte = np.frexp(amax)[1] - 1 + 127 - 7
    else:
        mant, ex = np.frexp(amax / 6.0)
        byte = np.where(mant > 0.5, ex, ex - 1) + 127
    byte = np.clip(np.where(amax > 0, byte, 1), 1, 254)
    scaled = (w * np.exp2(127.0 - byte)[:, None, :]).reshape(k, n).astype(np.float32)
    by_word = np.ascontiguousarray(scaled.reshape(k // 512, 128, 4, n).transpose(0, 1, 3, 2))
    if fmt == "e4m3":
        words = by_word.astype(ml_dtypes.float8_e4m3fn).view(np.uint8)
    else:
        c = by_word.astype(ml_dtypes.float4_e2m1fn).view(np.uint8) & 0xF
        words = (c[..., 0::2] | (c[..., 1::2] << 4)).reshape(k // 512, 128, 2 * n)
    return np.ascontiguousarray(words), np.ascontiguousarray(byte.astype(np.uint8).reshape(k // 512, 16, n))


def unpack_weight(words, scales, fmt):
    g, _, n = scales.shape
    words = np.ascontiguousarray(words).reshape(g, 128, n, -1)
    if fmt == "e4m3":
        vals = words.view(ml_dtypes.float8_e4m3fn).astype(np.float64)
    else:
        nib = np.empty((g, 128, n, 4), np.uint8)
        nib[..., 0::2] = words & 0xF
        nib[..., 1::2] = words >> 4
        vals = E2M1[nib]
    vals = vals * np.repeat(np.exp2(scales.astype(np.float64) - 127.0), 8, axis=1)[..., None]
    return vals.transpose(0, 1, 3, 2).reshape(g * 512, n)


def gelu(v):
    return 0.5 * v * (1.0 + np.tanh(np.sqrt(2.0 / np.pi) * (v + 0.044715 * v**3)))


K, H, T, S, T2, P = 1536, 1024, 2048, 1024, 2048, 512

def setup_inputs():
    n = np.random.standard_normal
    s = mx_kscale(K)[:, None]
    u = mx_kscale(H)[:, None]
    d = {}
    d["tab_words"], d["tab_scales"] = pack_weight(n((K, T)) * s, "e4m3")
    d["offs"] = striped(np.random.permutation(T)[:S])
    d["offs2"] = striped(np.random.permutation(T2)[:S])
    d["offs3"] = striped(np.random.permutation(T2)[:P])
    d["offs4"] = striped(np.random.permutation(T2)[:P])
    d["w1"] = (n((K, H)) / K ** 0.5 / s).astype(np.float32)
    d["gain"] = (np.exp(0.3 * n(H)) * u[:, 0]).astype(np.float32)
    d["wgs"] = np.exp(0.3 * n((128, S))).astype(np.float32)
    d["page0"] = (n((H, T2)) * u).astype(np.float32)
    d["cold"] = (1.3 * np.exp(0.2 * n(H)) / u[:, 0]).astype(np.float32)
    d["lift"] = (np.exp(0.3 * n(H)) * u[:, 0]).astype(np.float32)
    d["w2_words"], d["w2_scales"] = pack_weight(1.5 * n((H, H)) / H ** 0.5 / u, "e2m1")
    d["opp"] = (np.exp(0.3 * n(H)) / u[:, 0]).astype(np.float32)
    d["mat"] = n((H, P)).astype(np.float32)
    return d

def reference(tab_words, tab_scales, offs, offs2, offs3, offs4, w1, gain, wgs, page0, cold, lift, w2_words, w2_scales, opp, mat):
    v = unpack_weight(tab_words, tab_scales, "e4m3")[:, unstriped(offs)]
    h = (mxq(f64(w1), 0, "e4m3").T @ v) * f64(gain)[:, None]
    page = f64(page0).copy()
    page[:, unstriped(offs2)] = np.tile(f64(wgs), (H // 128, 1)) * h
    x = np.tanh(page[:, unstriped(offs3)] * f64(cold)[:, None]) * f64(lift)[:, None]
    w2 = unpack_weight(w2_words, w2_scales, "e2m1")
    y = w2.T @ mxq(x, 0, "e4m3")
    o = page[:, unstriped(offs4)] * f64(opp)[:, None]
    return np.maximum(y, o) * f64(mat)

from contextlib import ExitStack

import concourse.mybir as mybir
from concourse.masks import make_identity

K, H, T, S, T2, M = 1536, 1024, 2048, 1024, 2048, 512
FLOPS = 2 * K * H * S + 2 * H * H * M

F32 = mybir.dt.float32
BF16 = mybir.dt.bfloat16
I32 = mybir.dt.int32
U32 = mybir.dt.uint32
U16 = mybir.dt.uint16
U8 = mybir.dt.uint8
FP8X4 = mybir.dt.float8_e4m3fn_x4
FP4X4 = mybir.dt.float4_e2m1fn_x4
ACT = mybir.ActivationFunctionType
ALU = mybir.AluOpType

P = 128
PACK = 4
K_PASS = P * PACK
PASSES1 = K // K_PASS
PASSES2 = H // K_PASS
TILES = H // P
BANK = 512
W1_CHUNKS = (1, 1, 2, 2, 2)
GPSIMD_TILES = 6


def tile_list_tuyere_heat_page_kernel(
    tc, tab_words, tab_scales, offs, offs2, offs3, offs4, w1, gain, wgs, page0, cold, lift, w2_words, w2_scales, opp, mat, out
):
    nc = tc.nc
    with ExitStack() as ctx:
        lists = ctx.enter_context(tc.tile_pool(name="lists", bufs=1))
        keep = ctx.enter_context(tc.tile_pool(name="keep", bufs=1))
        ring = ctx.enter_context(tc.tile_pool(name="ring", bufs=2))
        psum = ctx.enter_context(tc.psum_pool(name="psum", bufs=1))

        def bank(number, shape, dtype, name):
            return psum.tile(shape, dtype, name=name, tag="bank%d" % number)

        idx = lists.tile([P, S // 16], U16, name="idx")
        idx2 = lists.tile([P, S // 16], U16, name="idx2")
        idx3 = lists.tile([P, M // 16], U16, name="idx3")
        idx4 = lists.tile([P, M // 16], U16, name="idx4")

        tab_s = keep.tile([P, T], U8, name="tab_s", align_bytes=64)
        nc.vector.memset(tab_s[:].bitcast(I32), 0)
        gain_rows = keep.tile([P, P], F32, name="gain_rows")
        late_rows = keep.tile([P, P], F32, name="late_rows")
        w2_s = keep.tile([P, PASSES2, H], U8, name="w2_s", align_bytes=64)
        nc.gpsimd.memset(gain_rows[:], 0.0)
        nc.vector.memset(late_rows[:], 0.0)
        nc.vector.memset(w2_s[:].rearrange("p a n -> p (a n)").bitcast(I32), 0)
        ident32 = keep.tile([P, P], F32, name="ident32")
        ident16 = keep.tile([P, P], BF16, name="ident16")
        make_identity(nc, ident32[:])
        make_identity(nc, ident16[:])

        tab_w = [keep.tile([P, T], U32, name="tab_w%d" % a, tag="table", bufs=PASSES1) for a in range(PASSES1)]
        pages = [keep.tile([P, T2], F32, name="page%d" % c) for c in range(TILES)]
        wgs_sb = keep.tile([P, S], F32, name="wgs_sb", tag="wgs")
        w2_w = keep.tile([P, PASSES2, 2 * H], U8, name="w2_w", align_bytes=64)
        first_tile = [sum(W1_CHUNKS[:i]) for i in range(len(W1_CHUNKS))]
        w1_raw = {}

        def load_table(a):
            nc.sync.dma_start(out=tab_w[a][:].bitcast(I32), in_=tab_words[a].rearrange("p t i -> p (t i)").bitcast(I32))

        def load_w1(chunk):
            width = W1_CHUNKS[chunk] * P
            cols = slice(first_tile[chunk] * P, first_tile[chunk] * P + width)
            raw = ring.tile([P, PASSES1 * PACK * width], F32, name="w1_raw", tag="w1_raw")
            for a in range(PASSES1):
                nc.sync.dma_start(
                    out=raw[:, a * PACK * width : (a + 1) * PACK * width].rearrange("p (j w) -> p j w", j=PACK),
                    in_=w1[a * K_PASS : (a + 1) * K_PASS, cols].rearrange("(p j) w -> p j w", j=PACK),
                )
            w1_raw[chunk] = raw

        def load_page(c):
            nc.sync.dma_start(out=pages[c][:], in_=page0[c * P : (c + 1) * P, :])

        nc.sync.dma_start(idx[:], offs)
        load_table(0)
        load_table(1)
        nc.sync.dma_start(out=gain_rows[0:TILES, :], in_=gain.rearrange("(c p) -> c p", p=P))
        for q in range(4):
            nc.sync.dma_start(
                out=tab_s[32 * q : 32 * q + 4 * PASSES1, :].bitcast(I32), in_=tab_scales[:, 4 * q : 4 * q + 4, :].bitcast(I32)
            )
        load_w1(0)
        nc.sync.dma_start(idx2[:], offs2)
        nc.sync.dma_start(out=wgs_sb[:, 0:BANK], in_=wgs[:, 0:BANK])
        load_table(2)
        load_page(0)
        load_w1(1)
        nc.sync.dma_start(out=wgs_sb[:, BANK:S], in_=wgs[:, BANK:S])
        nc.sync.dma_start(idx3[:], offs3)
        for v, vector in enumerate((cold, lift, opp)):
            nc.sync.dma_start(out=late_rows[v * TILES : (v + 1) * TILES, :], in_=vector.rearrange("(c p) -> c p", p=P))
        for c in range(1, TILES - 1):
            if c + 1 in first_tile:
                load_w1(first_tile.index(c + 1))
            load_page(c)
        nc.sync.dma_start(idx4[:], offs4)
        for q in range(4):
            nc.sync.dma_start(
                out=w2_s[32 * q : 32 * q + 4, :, :].bitcast(I32),
                in_=w2_scales[:, 4 * q : 4 * q + 4, :].rearrange("a r n -> r a n").bitcast(I32),
            )
        nc.sync.dma_start(out=w2_w[:].bitcast(I32), in_=w2_words.rearrange("a p n -> p a n").bitcast(I32))
        mats = []
        for half in range(2):
            mat_sb = keep.tile([P, TILES // 2, M], F32, name="mat%d" % half, tag="table", bufs=PASSES1)
            nc.sync.dma_start(out=mat_sb[:], in_=mat[half * K_PASS : (half + 1) * K_PASS, :].rearrange("(c p) m -> p c m", p=P))
            mats.append(mat_sb)
        load_page(TILES - 1)

        def staging_end(c):
            raw = w1_raw[first_tile.index(c)]
            return raw[:, raw.shape[1] - S - M : raw.shape[1]]

        gain_ps = bank(2, [P, P], F32, "gain_ps")
        nc.tensor.transpose(gain_ps[:], gain_rows[:], ident32[:])
        gain_col = keep.tile([P, TILES], F32, name="gain_col")
        nc.scalar.copy(gain_col[:], gain_ps[:, 0:TILES])

        v_w = [keep.tile([P, S], U32, name="v_w%d" % a, align_bytes=64) for a in range(PASSES1)]
        v_s = keep.tile([P, S], U8, name="v_s", align_bytes=64)
        nc.vector.tensor_copy(v_w[0][:], tab_w[0][:].indirect(idx[:]))
        nc.vector.tensor_copy(v_w[1][:], tab_w[1][:].indirect(idx[:]))
        nc.vector.tensor_copy(v_s[:], tab_s[:].indirect(idx[:]))

        w1_q = {}

        def quantize_w1(chunk):
            width = W1_CHUNKS[chunk] * P
            grouped = ring.tile([P, PASSES1, width, PACK], BF16, name="w1_bf", tag="w1_bf", align_bytes=64)
            for a in range(PASSES1):
                nc.scalar.copy(
                    grouped[:, a, :, :].rearrange("p (c i) j -> p c j i", i=4),
                    w1_raw[chunk][:, a * PACK * width : (a + 1) * PACK * width].rearrange("p (j c i) -> p c j i", j=PACK, i=4),
                )
            codes = ring.tile([P, PASSES1 * width], U32, name="w1_codes", tag="codes", align_bytes=64)
            scales = ring.tile([P, PASSES1 * width], U8, name="w1_scales", tag="scales", align_bytes=64)
            flat = grouped[:].rearrange("p a w j -> p (a w j)")
            for lo, hi in ((0, 2 * width), (2 * width, 3 * width)):
                nc.vector.quantize_mx(out=codes[:, lo:hi].bitcast(FP8X4), scales=scales[:, lo:hi], in_=flat[:, PACK * lo : PACK * hi])
            for t in range(W1_CHUNKS[chunk]):
                w1_q[first_tile[chunk] + t] = (codes, scales, width, t)

        def replace_columns(c):
            codes, scales, width, t = w1_q[c]
            if c > 0 and c + 1 in first_tile:
                h = staging_end(c + 1)[:, 0:S]
            else:
                h = ring.tile([P, S], F32, name="h", tag="h", bufs=6)[:]
            h_half = [h[:, 0:BANK], h[:, BANK:S] if c > 0 else staging_end(1)[:, S : S + M]]
            for half in range(2):
                cols = slice(half * BANK, (half + 1) * BANK)
                if c == 0 and half == 1:
                    quantize_w1(1)
                acc = bank(half if c > 0 else 0, [P, BANK], F32, "h_ps")
                for a in range(PASSES1):
                    rows = slice(a * width + t * P, a * width + (t + 1) * P)
                    nc.tensor.matmul_mx(
                        out=acc[:],
                        lhsT=codes[:, rows].bitcast(FP8X4),
                        lhsT_scale=scales[:, rows],
                        rhs=v_w[a][:, cols].bitcast(FP8X4),
                        rhs_scale=v_s[4 * a : P, cols],
                        start=(a == 0),
                        stop=(a == PASSES1 - 1),
                    )
                nc.scalar.activation(h_half[half], acc[:], ACT.Copy, scale=gain_col[:, c : c + 1])
                if c == 0:
                    nc.vector.tensor_tensor(
                        pages[c][:].indirect(idx2[:, half * 32 : (half + 1) * 32]), h_half[half], wgs_sb[:, cols], ALU.mult
                    )
            if c > 0:
                nc.vector.tensor_tensor(pages[c][:].indirect(idx2[:]), h, wgs_sb[:], ALU.mult)

        quantize_w1(0)
        for half in range(2):
            nc.vector.tensor_copy(
                v_w[2][:, half * BANK : (half + 1) * BANK], tab_w[2][:].indirect(idx[:, half * 32 : (half + 1) * 32])
            )
        for c in range(TILES):
            if c > 0 and c + 1 in first_tile:
                quantize_w1(first_tile.index(c + 1))
            replace_columns(c)

        late_ps = bank(2, [P, P], F32, "late_ps")
        nc.tensor.transpose(late_ps[:], late_rows[:], ident32[:])
        late_col = keep.tile([P, 3 * TILES], F32, name="late_col")
        nc.scalar.copy(late_col[:], late_ps[:, 0 : 3 * TILES])

        x_codes, x_scales, x_grouped = [], [], []
        for b in range(PASSES2):
            x_t = keep.tile([P, 4, 2, P], F32, name="x_t%d" % b)
            for t in range(4):
                c = 4 * b + t
                if c + 2 in first_tile:
                    picked = staging_end(c + 2)[:, S : S + M]
                else:
                    picked = ring.tile([P, M], F32, name="picked", tag="picked")[:]
                nc.vector.tensor_copy(picked, pages[c][:].indirect(idx3[:]))
                th = ring.tile([P, M], F32, name="th", tag="th")
                nc.scalar.activation(th[:], picked, ACT.Tanh, scale=late_col[:, c : c + 1])
                xb = ring.tile([P, M], BF16, name="xb", tag="xb")
                nc.scalar.activation(xb[:], th[:], ACT.Copy, scale=late_col[:, TILES + c : TILES + c + 1])
                turned = bank(2, [P, 4, P], BF16, "turned")
                for ch in range(4):
                    nc.tensor.transpose(turned[:, ch, :], xb[:, ch * P : (ch + 1) * P], ident16[:])
                nc.scalar.copy(
                    x_t[:, :, :, 32 * t : 32 * (t + 1)],
                    turned[:].rearrange("m ch r -> m (ch r)").bitcast(F32).rearrange("m (ch q u) -> m ch u q", ch=4, u=2),
                )
            grouped = keep.tile([P, M * PACK], BF16, name="x_bf%d" % b, tag="x_bf%d" % b, align_bytes=64)
            codes = ring.tile([P, M], U32, name="x_codes", tag="codes", align_bytes=64)
            scales = ring.tile([P, M], U8, name="x_scales", tag="scales", align_bytes=64)
            for j in range(2):
                back = bank(3 + j, [P, 2, 2, P], F32, "back")
                for ch in range(2):
                    for u in range(2):
                        nc.tensor.transpose(back[:, ch, u, :], x_t[:, 2 * j + ch, u, :], ident32[:])
                part = grouped[:, j * 1024 : (j + 1) * 1024]
                nc.scalar.copy(
                    part.bitcast(F32).rearrange("p (ch m u) -> p ch m u", ch=2, u=2), back[:].rearrange("p ch u m -> p ch m u")
                )
                nc.vector.quantize_mx(
                    out=codes[:, j * 256 : (j + 1) * 256].bitcast(FP8X4), scales=scales[:, j * 256 : (j + 1) * 256], in_=part
                )
            x_codes.append(codes)
            x_scales.append(scales)

        y_banks = (5, 6, 7, 0, 1, 2, 3, 4)
        ys = [bank(y_banks[n], [P, M], F32, "y%d" % n) for n in range(TILES)]

        def y_pass(n, b):
            nc.tensor.matmul_mx(
                out=ys[n][:],
                lhsT=w2_w[:, b, 2 * P * n : 2 * P * (n + 1)].bitcast(FP4X4),
                lhsT_scale=w2_s[:, b, P * n : P * (n + 1)],
                rhs=x_codes[b][:].bitcast(FP8X4),
                rhs_scale=x_scales[b][:],
                start=(b == 0),
                stop=(b == PASSES2 - 1),
            )

        early = keep.tile([P, 4, M], F32, name="opp_early", tag="wgs")
        fifth = keep.tile([P, M], F32, name="opp_fifth", tag="x_bf1", align_bytes=64)
        opposite = [early[:, n, :] for n in range(4)] + [fifth[:]] + [early[:, n, :] for n in range(3)]

        def gather_opposite(n):
            nc.vector.tensor_copy(opposite[n], pages[n][:].indirect(idx4[:]))

        for n in range(5):
            y_pass(n, 0)
            gather_opposite(n)
        for n in range(TILES):
            if n >= 5:
                y_pass(n, 0)
            y_pass(n, 1)
            larger = ring.tile([P, M], F32, name="larger", tag="larger", bufs=4)
            nc.vector.scalar_tensor_tensor(
                larger[:], opposite[n], late_col[:, 2 * TILES + n : 2 * TILES + n + 1], ys[n][:], ALU.mult, ALU.max
            )
            if 1 <= n <= 3:
                gather_opposite(n + 4)
            result = ring.tile([P, M], F32, name="result", tag="h", bufs=6)
            engine = nc.gpsimd if n < GPSIMD_TILES else nc.vector
            engine.tensor_tensor(result[:], larger[:], mats[n // 4][:, n % 4, :], ALU.mult)
            nc.sync.dma_start(out=out[n * P : (n + 1) * P, :], in_=result[:])
